import numpy as np
import ml_dtypes


def mxq(x, axis, fmt="e4m3"):
    dtype, down = {"e4m3": (ml_dtypes.float8_e4m3fn, 7), "e5m2": (ml_dtypes.float8_e5m2, 14)}[fmt]
    v = np.moveaxis(np.asarray(x, np.float32).astype(ml_dtypes.bfloat16).astype(np.float64), axis, -1)
    blocks = v.reshape(v.shape[:-1] + (-1, 32))
    amax = np.abs(blocks).max(-1, keepdims=True)
    byte = np.maximum(np.where(amax > 0, np.frexp(amax)[1] - 1 + 127, 0) - down, 1)
    scale = np.exp2(byte - 127.0)
    codes = (blocks / scale).astype(np.float32).astype(dtype).astype(np.float64)
    return np.moveaxis((codes * scale).reshape(v.shape), -1, axis)


WIDE = False


def mx_kscale(k):
    if not WIDE:
        return np.ones(k)
    levels = np.array([10, -10, 5, -5, 0])
    if k % 512:
        return np.exp2(np.random.permutation(np.resize(levels, k // 32))).repeat(32)
    a = np.empty((k // 512, 16))
    for p in range(k // 512):
        a[p, :8] = np.random.permutation(np.resize(levels, 8))
        for g in range(8):
            far = levels[np.abs(levels - a[p, g]) >= 10]
            a[p, g + 8] = far[np.random.randint(len(far))]
    return np.exp2(a.ravel()).repeat(32)


def f64(x):
    return np.asarray(x).astype(np.float64)


def striped(idx):
    return np.tile(np.asarray(idx).reshape(-1, 16).T, (8, 1)).astype(np.uint16)


def unstriped(offs):
    return offs[:16].T.reshape(-1).astype(np.int64)


E2M1 = np.array([0.0, 0.5, 1.0, 1.5, 2.0, 3.0, 4.0, 6.0, -0.0, -0.5, -1.0, -1.5, -2.0, -3.0, -4.0, -6.0])


def pack_weight(w, fmt):
    k, n = w.shape
    w = f64(np.asarray(w, np.float32).astype(ml_dtypes.bfloat16)).reshape(k // 32, 32, n)
    amax = np.abs(w).max(1)
    if fmt == "e4m3":
        byte = np.frexp(amax)[1] - 1 + 127 - 7
    else:
        mant, ex = np.frexp(amax / 6.0)
        byte = np.where(mant > 0.5, ex, ex - 1) + 127
    byte = np.clip(np.where(amax > 0, byte, 1), 1, 254)
    scaled = (w * np.exp2(127.0 - byte)[:, None, :]).reshape(k, n).astype(np.float32)
    by_word = np.ascontiguousarray(scaled.reshape(k // 512, 128, 4, n).transpose(0, 1, 3, 2))
    if fmt == "e4m3":
        words = by_word.astype(ml_dtypes.float8_e4m3fn).view(np.uint8)
    else:
        c = by_word.astype(ml_dtypes.float4_e2m1fn).view(np.uint8) & 0xF
        words = (c[..., 0::2] | (c[..., 1::2] << 4)).reshape(k // 512, 128, 2 * n)
    return np.ascontiguousarray(words), np.ascontiguousarray(byte.astype(np.uint8).reshape(k // 512, 16, n))


def unpack_weight(words, scales, fmt):
    g, _, n = scales.shape
    words = np.ascontiguousarray(words).reshape(g, 128, n, -1)
    if fmt == "e4m3":
        vals = words.view(ml_dtypes.float8_e4m3fn).astype(np.float64)
    else:
        nib = np.empty((g, 128, n, 4), np.uint8)
        nib[..., 0::2] = words & 0xF
        nib[..., 1::2] = words >> 4
        vals = E2M1[nib]
    vals = vals * np.repeat(np.exp2(scales.astype(np.float64) - 127.0), 8, axis=1)[..., None]
    return vals.transpose(0, 1, 3, 2).reshape(g * 512, n)


B, N, T, D, NQ = 1, 512, 2048, 512, 256


def setup_inputs():
    n = np.random.standard_normal
    idx = np.random.permutation(T)[:B * N]
    idx2 = np.random.permutation(1024)[:B * N]
    s = mx_kscale(D)[:, None]
    kp = pack_weight(n((D, T)) / s, "e4m3")
    cp = pack_weight(n((D, 1024)) / s, "e4m3")
    return {
        "uT": (n((B, D, NQ)) * s * (1.00 / np.sqrt(D))).astype(np.float32),
        "vT": (n((B, D, NQ)) * s * (1.00 / np.sqrt(D))).astype(np.float32),
        "k_words": kp[0],
        "k_scales": kp[1],
        "c_words": cp[0],
        "c_scales": cp[1],
        "offs": striped(idx),
        "offs2": striped(idx2),
    }


def reference(uT, vT, k_words, k_scales, c_words, c_scales, offs, offs2):
    idx = unstriped(offs)
    idx2 = unstriped(offs2)
    pick = lambda x, which: x[:, which].reshape(x.shape[0], B, -1).transpose(1, 0, 2)
    k = unpack_weight(k_words, k_scales, "e4m3")
    kg = pick(k, idx)
    c = unpack_weight(c_words, c_scales, "e4m3")
    cg = pick(c, idx2)
    uq = mxq(f64(uT), 1, "e4m3")
    vq = mxq(f64(vT), 1, "e4m3")
    a = (uq.transpose(0, 2, 1) @ kg) + (vq.transpose(0, 2, 1) @ cg)
    return a

@@ -1,0 +1,115 @@
+from contextlib import ExitStack
+
+import concourse.mybir as mybir
+
+F32 = mybir.dt.float32
+BF16 = mybir.dt.bfloat16
+I32 = mybir.dt.int32
+U32 = mybir.dt.uint32
+U16 = mybir.dt.uint16
+U8 = mybir.dt.uint8
+FP8X4 = mybir.dt.float8_e4m3fn_x4
+
+P = 128
+PACK = 4
+D, NQ, SLOTS, T_KEYS, T_POS = 512, 256, 512, 2048, 1024
+PART = 128
+PARTS = SLOTS // PART
+Q_TILES = NQ // P
+FLOPS = 2 * 2 * D * NQ * SLOTS
+
+
+def interleave(copy, grouped, raw):
+    copy(out=grouped.rearrange("p (c i) t -> p c t i", i=4), in_=raw.rearrange("p t (c i) -> p c t i", i=4))
+
+
+def tile_attend_txl_topk_kernel(tc, uT, vT, k_words, k_scales, c_words, c_scales, offs, offs2, out):
+    nc = tc.nc
+    with ExitStack() as ctx:
+        sb = ctx.enter_context(tc.tile_pool(name="sb", bufs=1))
+        psum = ctx.enter_context(tc.psum_pool(name="psum", bufs=1))
+
+        k_list = sb.tile([P, SLOTS // 16], U16, name="k_list")
+        c_list = sb.tile([P, SLOTS // 16], U16, name="c_list")
+        k_bytes = sb.tile([P, T_KEYS], U8, name="k_bytes", align_bytes=64)
+        c_bytes = sb.tile([P, T_POS], U8, name="c_bytes", align_bytes=64)
+        planes = sb.tile([P, 2 * SLOTS], U8, name="planes", align_bytes=64)
+        nc.vector.memset(k_bytes[:].bitcast(I32), 0)
+        nc.vector.memset(c_bytes[:].bitcast(I32), 0)
+        nc.vector.memset(planes[:].bitcast(I32), 0)
+
+        u_raw = sb.tile([P, PACK, NQ], F32, name="u_raw")
+        v_raw = sb.tile([P, PACK, NQ], F32, name="v_raw")
+        k_pool = sb.tile([P, T_KEYS], U32, name="k_pool", align_bytes=64)
+        c_pool = sb.tile([P, T_POS], U32, name="c_pool", align_bytes=64)
+
+        nc.sync.dma_start(k_list[:], offs)
+        nc.sync.dma_start(out=u_raw[:], in_=uT[0].rearrange("(p t) q -> p t q", t=PACK))
+        nc.sync.dma_start(c_list[:], offs2)
+        nc.scalar.dma_start(out=k_bytes[0:P:8, :].bitcast(I32), in_=k_scales[0].bitcast(I32))
+        nc.scalar.dma_start(out=c_bytes[0:P:8, :].bitcast(I32), in_=c_scales[0].bitcast(I32))
+        nc.sync.dma_start(out=k_pool[:].bitcast(I32), in_=k_words[0].rearrange("p n t -> p (n t)").bitcast(I32))
+        nc.sync.dma_start(out=v_raw[:], in_=vT[0].rearrange("(p t) q -> p t q", t=PACK))
+        nc.sync.dma_start(out=c_pool[:].bitcast(I32), in_=c_words[0].rearrange("p n t -> p (n t)").bitcast(I32))
+
+        picked = sb.tile([P, 2 * SLOTS], U8, name="picked", align_bytes=64)
+        nc.vector.tensor_copy(picked[:, 0:SLOTS], k_bytes[:].indirect(k_list[:]))
+        nc.vector.tensor_copy(picked[:, SLOTS : 2 * SLOTS], c_bytes[:].indirect(c_list[:]))
+
+        u_bf = sb.tile([P, NQ, PACK], BF16, name="u_bf", align_bytes=64)
+        interleave(nc.scalar.copy, u_bf[:], u_raw[:])
+        for quad in range(4):
+            nc.scalar.dma_start(
+                out=planes[32 * quad : 32 * quad + 4, :].bitcast(I32),
+                in_=picked[32 * quad : 32 * quad + 32 : 8, :].bitcast(I32),
+            )
+        u_codes = sb.tile([P, NQ], U32, name="u_codes", align_bytes=64)
+        u_plane = sb.tile([P, NQ], U8, name="u_plane", align_bytes=64)
+        nc.vector.quantize_mx(out=u_codes[:].bitcast(FP8X4), scales=u_plane[:], in_=u_bf[:].rearrange("p q t -> p (q t)"))
+
+        k_got = sb.tile([P, SLOTS], U32, name="k_got", align_bytes=64)
+        nc.vector.tensor_copy(k_got[:], k_pool[:].indirect(k_list[:]))
+
+        banks = [[psum.tile([P, PART], F32, name="acc%d_%d" % (j, m)) for m in range(Q_TILES)] for j in range(PARTS)]
+        for j in range(PARTS):
+            cols = slice(j * PART, (j + 1) * PART)
+            for m in range(Q_TILES):
+                rows = slice(m * P, (m + 1) * P)
+                nc.tensor.matmul_mx(
+                    out=banks[j][m][:],
+                    lhsT=u_codes[:, rows].bitcast(FP8X4),
+                    lhsT_scale=u_plane[:, rows],
+                    rhs=k_got[:, cols].bitcast(FP8X4),
+                    rhs_scale=planes[:, cols],
+                    start=True,
+                    stop=False,
+                )
+
+        v_codes = []
+        v_plane = []
+        for m, copy in enumerate((nc.vector.tensor_copy, nc.scalar.copy)):
+            v_bf = sb.tile([P, P, PACK], BF16, name="v_bf%d" % m, align_bytes=64)
+            interleave(copy, v_bf[:], v_raw[:, :, m * P : (m + 1) * P])
+            v_codes.append(sb.tile([P, P], U32, name="v_codes%d" % m, align_bytes=64))
+            v_plane.append(sb.tile([P, P], U8, name="v_plane%d" % m, align_bytes=64))
+            nc.vector.quantize_mx(out=v_codes[m][:].bitcast(FP8X4), scales=v_plane[m][:], in_=v_bf[:].rearrange("p q t -> p (q t)"))
+
+        out_view = out[0].rearrange("(m p) n -> p m n", p=P)
+        for j in range(PARTS):
+            cols = slice(j * PART, (j + 1) * PART)
+            c_got = sb.tile([P, PART], U32, name="c_got%d" % j, align_bytes=64)
+            nc.vector.tensor_copy(c_got[:], c_pool[:].indirect(c_list[:, j * PART // 16 : (j + 1) * PART // 16]))
+            result = sb.tile([P, Q_TILES, PART], F32, name="result%d" % j)
+            for m in range(Q_TILES):
+                nc.tensor.matmul_mx(
+                    out=banks[j][m][:],
+                    lhsT=v_codes[m][:].bitcast(FP8X4),
+                    lhsT_scale=v_plane[m][:],
+                    rhs=c_got[:].bitcast(FP8X4),
+                    rhs_scale=planes[:, SLOTS + j * PART : SLOTS + (j + 1) * PART],
+                    start=False,
+                    stop=True,
+                )
+                copy = nc.vector.tensor_copy if (j == PARTS - 1 and m == Q_TILES - 1) else nc.scalar.copy
+                copy(out=result[:, m, :], in_=banks[j][m][:])
+            nc.sync.dma_start(out=out_view[:, :, cols], in_=result[:])

@@ -13,14 +13,9 @@ FP8X4 = mybir.dt.float8_e4m3fn_x4
 P = 128
 PACK = 4
 D, NQ, SLOTS, T_KEYS, T_POS = 512, 256, 512, 2048, 1024
-PART = 128
-PARTS = SLOTS // PART
-Q_TILES = NQ // P
+PARTS = (((0, 256), (256, 512)), ((0, 256), (256, 384), (384, 512)))
+ROW0 = P - 16
 FLOPS = 2 * 2 * D * NQ * SLOTS
-
-
-def interleave(copy, grouped, raw):
-    copy(out=grouped.rearrange("p (c i) t -> p c t i", i=4), in_=raw.rearrange("p t (c i) -> p c t i", i=4))
 
 
 def tile_attend_txl_topk_kernel(tc, uT, vT, k_words, k_scales, c_words, c_scales, offs, offs2, out):
@@ -29,87 +24,93 @@ def tile_attend_txl_topk_kernel(tc, uT, vT, k_words, k_scales, c_words, c_scales
         sb = ctx.enter_context(tc.tile_pool(name="sb", bufs=1))
         psum = ctx.enter_context(tc.psum_pool(name="psum", bufs=1))
 
+        def round_queries(name, raw, *copies):
+            grouped = sb.tile([P, P, PACK], BF16, name=name, align_bytes=64)
+            share = P // len(copies)
+            for n, copy in enumerate(copies):
+                rows = slice(n * share, (n + 1) * share)
+                copy(out=grouped[:, rows, :].rearrange("p (c i) t -> p c t i", i=4), in_=raw[:, :, rows].rearrange("p t (c i) -> p c t i", i=4))
+            return grouped
+
+        def quantise_queries(name, grouped):
+            codes = sb.tile([P, P], U32, name=name + "_codes", align_bytes=64)
+            plane = sb.tile([P, P], U8, name=name + "_plane", align_bytes=64)
+            nc.vector.quantize_mx(out=codes[:].bitcast(FP8X4), scales=plane[:], in_=grouped[:].rearrange("p q t -> p (q t)"))
+            return codes, plane
+
         k_list = sb.tile([P, SLOTS // 16], U16, name="k_list")
         c_list = sb.tile([P, SLOTS // 16], U16, name="c_list")
         k_bytes = sb.tile([P, T_KEYS], U8, name="k_bytes", align_bytes=64)
-        c_bytes = sb.tile([P, T_POS], U8, name="c_bytes", align_bytes=64)
+        c_bytes = sb.tile([P, T_POS], U8, name="c_bytes", tag="late_room", align_bytes=64)
         planes = sb.tile([P, 2 * SLOTS], U8, name="planes", align_bytes=64)
-        nc.vector.memset(k_bytes[:].bitcast(I32), 0)
-        nc.vector.memset(c_bytes[:].bitcast(I32), 0)
+        nc.vector.memset(k_bytes[0:ROW0, :].bitcast(I32), 0)
+        nc.vector.memset(c_bytes[0:ROW0, :].bitcast(I32), 0)
         nc.vector.memset(planes[:].bitcast(I32), 0)
 
-        u_raw = sb.tile([P, PACK, NQ], F32, name="u_raw")
-        v_raw = sb.tile([P, PACK, NQ], F32, name="v_raw")
         k_pool = sb.tile([P, T_KEYS], U32, name="k_pool", align_bytes=64)
         c_pool = sb.tile([P, T_POS], U32, name="c_pool", align_bytes=64)
 
+        u_raw = sb.tile([P, PACK, NQ], F32, name="u_raw")
         nc.sync.dma_start(k_list[:], offs)
-        nc.sync.dma_start(out=u_raw[:], in_=uT[0].rearrange("(p t) q -> p t q", t=PACK))
+        nc.scalar.dma_start(out=k_bytes[ROW0:P, :].bitcast(I32), in_=k_scales[0].bitcast(I32))
         nc.sync.dma_start(c_list[:], offs2)
-        nc.scalar.dma_start(out=k_bytes[0:P:8, :].bitcast(I32), in_=k_scales[0].bitcast(I32))
-        nc.scalar.dma_start(out=c_bytes[0:P:8, :].bitcast(I32), in_=c_scales[0].bitcast(I32))
+        nc.scalar.dma_start(out=c_bytes[ROW0:P, :].bitcast(I32), in_=c_scales[0].bitcast(I32))
+        nc.sync.dma_start(out=u_raw[:], in_=uT[0].rearrange("(p t) q -> p t q", t=PACK))
         nc.sync.dma_start(out=k_pool[:].bitcast(I32), in_=k_words[0].rearrange("p n t -> p (n t)").bitcast(I32))
-        nc.sync.dma_start(out=v_raw[:], in_=vT[0].rearrange("(p t) q -> p t q", t=PACK))
         nc.sync.dma_start(out=c_pool[:].bitcast(I32), in_=c_words[0].rearrange("p n t -> p (n t)").bitcast(I32))
+
+        warm_in = sb.tile([P, 1], F32, name="warm_in")
+        warm_out = sb.tile([P, 1], F32, name="warm_out")
+        nc.gpsimd.memset(warm_in[:], 0.0)
+        nc.scalar.copy(out=warm_out[:], in_=warm_in[:])
 
         picked = sb.tile([P, 2 * SLOTS], U8, name="picked", align_bytes=64)
         nc.vector.tensor_copy(picked[:, 0:SLOTS], k_bytes[:].indirect(k_list[:]))
         nc.vector.tensor_copy(picked[:, SLOTS : 2 * SLOTS], c_bytes[:].indirect(c_list[:]))
-
-        u_bf = sb.tile([P, NQ, PACK], BF16, name="u_bf", align_bytes=64)
-        interleave(nc.scalar.copy, u_bf[:], u_raw[:])
+        u0_bf = round_queries("u0_bf", u_raw[:, :, 0:P], nc.scalar.copy)
+        u1_bf = round_queries("u1_bf", u_raw[:, :, P:NQ], nc.scalar.copy)
         for quad in range(4):
-            nc.scalar.dma_start(
+            nc.sync.dma_start(
                 out=planes[32 * quad : 32 * quad + 4, :].bitcast(I32),
-                in_=picked[32 * quad : 32 * quad + 32 : 8, :].bitcast(I32),
+                in_=picked[ROW0 + 4 * quad : ROW0 + 4 * quad + 4, :].bitcast(I32),
             )
-        u_codes = sb.tile([P, NQ], U32, name="u_codes", align_bytes=64)
-        u_plane = sb.tile([P, NQ], U8, name="u_plane", align_bytes=64)
-        nc.vector.quantize_mx(out=u_codes[:].bitcast(FP8X4), scales=u_plane[:], in_=u_bf[:].rearrange("p q t -> p (q t)"))
+        v_raw = sb.tile([P, 2, PACK, P], F32, name="v_raw", tag="late_room", align_bytes=64)
+        for m in range(2):
+            nc.sync.dma_start(out=v_raw[:, m], in_=vT[0].rearrange("(p t) q -> p t q", t=PACK)[:, :, m * P : (m + 1) * P])
+        u0 = quantise_queries("u0", u0_bf)
+        u1 = quantise_queries("u1", u1_bf)
 
         k_got = sb.tile([P, SLOTS], U32, name="k_got", align_bytes=64)
         nc.vector.tensor_copy(k_got[:], k_pool[:].indirect(k_list[:]))
+        c_got = sb.tile([P, SLOTS], U32, name="c_got", align_bytes=64)
+        nc.vector.tensor_copy(c_got[:], c_pool[:].indirect(c_list[:]))
 
-        banks = [[psum.tile([P, PART], F32, name="acc%d_%d" % (j, m)) for m in range(Q_TILES)] for j in range(PARTS)]
-        for j in range(PARTS):
-            cols = slice(j * PART, (j + 1) * PART)
-            for m in range(Q_TILES):
-                rows = slice(m * P, (m + 1) * P)
+        v0_bf = round_queries("v0_bf", v_raw[:, 0], nc.scalar.copy)
+        v0 = quantise_queries("v0", v0_bf)
+        v1_bf = round_queries("v1_bf", v_raw[:, 1], nc.vector.tensor_copy, nc.scalar.copy)
+        v1 = quantise_queries("v1", v1_bf)
+
+        banks = [[psum.tile([P, hi - lo], F32, name="acc%d_%d" % (m, lo)) for lo, hi in PARTS[m]] for m in range(2)]
+
+        def product(m, queries, got, at, first):
+            codes, plane = queries
+            for j, (lo, hi) in enumerate(PARTS[m]):
                 nc.tensor.matmul_mx(
-                    out=banks[j][m][:],
-                    lhsT=u_codes[:, rows].bitcast(FP8X4),
-                    lhsT_scale=u_plane[:, rows],
-                    rhs=k_got[:, cols].bitcast(FP8X4),
-                    rhs_scale=planes[:, cols],
-                    start=True,
-                    stop=False,
+                    out=banks[m][j][:],
+                    lhsT=codes[:].bitcast(FP8X4),
+                    lhsT_scale=plane[:],
+                    rhs=got[:, lo:hi].bitcast(FP8X4),
+                    rhs_scale=planes[:, at + lo : at + hi],
+                    start=first,
+                    stop=not first,
                 )
 
-        v_codes = []
-        v_plane = []
-        for m, copy in enumerate((nc.vector.tensor_copy, nc.scalar.copy)):
-            v_bf = sb.tile([P, P, PACK], BF16, name="v_bf%d" % m, align_bytes=64)
-            interleave(copy, v_bf[:], v_raw[:, :, m * P : (m + 1) * P])
-            v_codes.append(sb.tile([P, P], U32, name="v_codes%d" % m, align_bytes=64))
-            v_plane.append(sb.tile([P, P], U8, name="v_plane%d" % m, align_bytes=64))
-            nc.vector.quantize_mx(out=v_codes[m][:].bitcast(FP8X4), scales=v_plane[m][:], in_=v_bf[:].rearrange("p q t -> p (q t)"))
-
-        out_view = out[0].rearrange("(m p) n -> p m n", p=P)
-        for j in range(PARTS):
-            cols = slice(j * PART, (j + 1) * PART)
-            c_got = sb.tile([P, PART], U32, name="c_got%d" % j, align_bytes=64)
-            nc.vector.tensor_copy(c_got[:], c_pool[:].indirect(c_list[:, j * PART // 16 : (j + 1) * PART // 16]))
-            result = sb.tile([P, Q_TILES, PART], F32, name="result%d" % j)
-            for m in range(Q_TILES):
-                nc.tensor.matmul_mx(
-                    out=banks[j][m][:],
-                    lhsT=v_codes[m][:].bitcast(FP8X4),
-                    lhsT_scale=v_plane[m][:],
-                    rhs=c_got[:].bitcast(FP8X4),
-                    rhs_scale=planes[:, SLOTS + j * PART : SLOTS + (j + 1) * PART],
-                    start=False,
-                    stop=True,
-                )
-                copy = nc.vector.tensor_copy if (j == PARTS - 1 and m == Q_TILES - 1) else nc.scalar.copy
-                copy(out=result[:, m, :], in_=banks[j][m][:])
-            nc.sync.dma_start(out=out_view[:, :, cols], in_=result[:])
+        product(0, u0, k_got, 0, True)
+        product(1, u1, k_got, 0, True)
+        for m, v in enumerate((v0, v1)):
+            product(m, v, c_got, SLOTS, False)
+            result = sb.tile([P, SLOTS], F32, name="result%d" % m, tag="late_room" if m == 0 else "result1", align_bytes=64)
+            for j, (lo, hi) in enumerate(PARTS[m]):
+                copy = nc.vector.tensor_copy if m == 1 and j != 1 else nc.scalar.copy
+                copy(out=result[:, lo:hi], in_=banks[m][j][:])
+                nc.sync.dma_start(out=out[0, m * P : (m + 1) * P, lo:hi], in_=result[:, lo:hi])

@@ -67,21 +67,34 @@ def tile_attend_txl_topk_kernel(tc, uT, vT, k_words, k_scales, c_words, c_scales
         picked = sb.tile([P, 2 * SLOTS], U8, name="picked", align_bytes=64)
         nc.vector.tensor_copy(picked[:, 0:SLOTS], k_bytes[:].indirect(k_list[:]))
         nc.vector.tensor_copy(picked[:, SLOTS : 2 * SLOTS], c_bytes[:].indirect(c_list[:]))
-        u0_bf = round_queries("u0_bf", u_raw[:, :, 0:P], nc.scalar.copy)
-        u1_bf = round_queries("u1_bf", u_raw[:, :, P:NQ], nc.scalar.copy)
         for quad in range(4):
-            nc.sync.dma_start(
+            queue = nc.scalar if quad % 2 else nc.sync
+            queue.dma_start(
                 out=planes[32 * quad : 32 * quad + 4, :].bitcast(I32),
                 in_=picked[ROW0 + 4 * quad : ROW0 + 4 * quad + 4, :].bitcast(I32),
             )
         v_raw = sb.tile([P, 2, PACK, P], F32, name="v_raw", tag="late_room", align_bytes=64)
         for m in range(2):
             nc.sync.dma_start(out=v_raw[:, m], in_=vT[0].rearrange("(p t) q -> p t q", t=PACK)[:, :, m * P : (m + 1) * P])
+        u0_bf = round_queries("u0_bf", u_raw[:, :, 0:P], nc.vector.tensor_copy)
+        u1_bf = round_queries("u1_bf", u_raw[:, :, P:NQ], nc.vector.tensor_copy)
         u0 = quantise_queries("u0", u0_bf)
         u1 = quantise_queries("u1", u1_bf)
 
         k_got = sb.tile([P, SLOTS], U32, name="k_got", align_bytes=64)
-        nc.vector.tensor_copy(k_got[:], k_pool[:].indirect(k_list[:]))
+        nc.vector.tensor_copy(k_got[:, 0:256], k_pool[:].indirect(k_list[:, 0:16]))
+        spare = psum.tile([P, 4, P], F32, name="spare")
+        for n in range(4):
+            nc.tensor.matmul_mx(
+                out=spare[:, n, :],
+                lhsT=u0[0][:].bitcast(FP8X4),
+                lhsT_scale=u0[1][:],
+                rhs=k_got[:, 0:P].bitcast(FP8X4),
+                rhs_scale=u1[1][:],
+                start=True,
+                stop=True,
+            )
+        nc.vector.tensor_copy(k_got[:, 256:512], k_pool[:].indirect(k_list[:, 16:32]))
         c_got = sb.tile([P, SLOTS], U32, name="c_got", align_bytes=64)
         nc.vector.tensor_copy(c_got[:], c_pool[:].indirect(c_list[:]))
 

from contextlib import ExitStack

import concourse.mybir as mybir

F32 = mybir.dt.float32
BF16 = mybir.dt.bfloat16
I32 = mybir.dt.int32
U32 = mybir.dt.uint32
U16 = mybir.dt.uint16
U8 = mybir.dt.uint8
FP8X4 = mybir.dt.float8_e4m3fn_x4

P = 128
PACK = 4
D, NQ, SLOTS, T_KEYS, T_POS = 512, 256, 512, 2048, 1024
PARTS = (((0, 256), (256, 512)), ((0, 256), (256, 384), (384, 512)))
ROW0 = P - 16
FLOPS = 2 * 2 * D * NQ * SLOTS


def tile_attend_txl_topk_kernel(tc, uT, vT, k_words, k_scales, c_words, c_scales, offs, offs2, out):
    nc = tc.nc
    with ExitStack() as ctx:
        sb = ctx.enter_context(tc.tile_pool(name="sb", bufs=1))
        psum = ctx.enter_context(tc.psum_pool(name="psum", bufs=1))

        def round_queries(name, raw, *copies):
            grouped = sb.tile([P, P, PACK], BF16, name=name, align_bytes=64)
            share = P // len(copies)
            for n, copy in enumerate(copies):
                rows = slice(n * share, (n + 1) * share)
                copy(out=grouped[:, rows, :].rearrange("p (c i) t -> p c t i", i=4), in_=raw[:, :, rows].rearrange("p t (c i) -> p c t i", i=4))
            return grouped

        def quantise_queries(name, grouped):
            codes = sb.tile([P, P], U32, name=name + "_codes", align_bytes=64)
            plane = sb.tile([P, P], U8, name=name + "_plane", align_bytes=64)
            nc.vector.quantize_mx(out=codes[:].bitcast(FP8X4), scales=plane[:], in_=grouped[:].rearrange("p q t -> p (q t)"))
            return codes, plane

        k_list = sb.tile([P, SLOTS // 16], U16, name="k_list")
        c_list = sb.tile([P, SLOTS // 16], U16, name="c_list")
        k_bytes = sb.tile([P, T_KEYS], U8, name="k_bytes", align_bytes=64)
        c_bytes = sb.tile([P, T_POS], U8, name="c_bytes", tag="late_room", align_bytes=64)
        planes = sb.tile([P, 2 * SLOTS], U8, name="planes", align_bytes=64)
        nc.vector.memset(k_bytes[0:ROW0, :].bitcast(I32), 0)
        nc.vector.memset(c_bytes[0:ROW0, :].bitcast(I32), 0)
        nc.vector.memset(planes[:].bitcast(I32), 0)

        k_pool = sb.tile([P, T_KEYS], U32, name="k_pool", align_bytes=64)
        c_pool = sb.tile([P, T_POS], U32, name="c_pool", align_bytes=64)

        u_raw = sb.tile([P, PACK, NQ], F32, name="u_raw")
        nc.sync.dma_start(k_list[:], offs)
        nc.scalar.dma_start(out=k_bytes[ROW0:P, :].bitcast(I32), in_=k_scales[0].bitcast(I32))
        nc.sync.dma_start(c_list[:], offs2)
        nc.scalar.dma_start(out=c_bytes[ROW0:P, :].bitcast(I32), in_=c_scales[0].bitcast(I32))
        nc.sync.dma_start(out=u_raw[:], in_=uT[0].rearrange("(p t) q -> p t q", t=PACK))
        nc.sync.dma_start(out=k_pool[:].bitcast(I32), in_=k_words[0].rearrange("p n t -> p (n t)").bitcast(I32))
        nc.sync.dma_start(out=c_pool[:].bitcast(I32), in_=c_words[0].rearrange("p n t -> p (n t)").bitcast(I32))

        warm_in = sb.tile([P, 1], F32, name="warm_in")
        warm_out = sb.tile([P, 1], F32, name="warm_out")
        nc.gpsimd.memset(warm_in[:], 0.0)
        nc.scalar.copy(out=warm_out[:], in_=warm_in[:])

        picked = sb.tile([P, 2 * SLOTS], U8, name="picked", align_bytes=64)
        nc.vector.tensor_copy(picked[:, 0:SLOTS], k_bytes[:].indirect(k_list[:]))
        nc.vector.tensor_copy(picked[:, SLOTS : 2 * SLOTS], c_bytes[:].indirect(c_list[:]))
        for quad in range(4):
            queue = nc.scalar if quad % 2 else nc.sync
            queue.dma_start(
                out=planes[32 * quad : 32 * quad + 4, :].bitcast(I32),
                in_=picked[ROW0 + 4 * quad : ROW0 + 4 * quad + 4, :].bitcast(I32),
            )
        v_raw = sb.tile([P, 2, PACK, P], F32, name="v_raw", tag="late_room", align_bytes=64)
        for m in range(2):
            nc.sync.dma_start(out=v_raw[:, m], in_=vT[0].rearrange("(p t) q -> p t q", t=PACK)[:, :, m * P : (m + 1) * P])
        u0_bf = round_queries("u0_bf", u_raw[:, :, 0:P], nc.vector.tensor_copy)
        u1_bf = round_queries("u1_bf", u_raw[:, :, P:NQ], nc.vector.tensor_copy)
        u0 = quantise_queries("u0", u0_bf)
        u1 = quantise_queries("u1", u1_bf)

        k_got = sb.tile([P, SLOTS], U32, name="k_got", align_bytes=64)
        nc.vector.tensor_copy(k_got[:, 0:256], k_pool[:].indirect(k_list[:, 0:16]))
        spare = psum.tile([P, 4, P], F32, name="spare")
        for n in range(4):
            nc.tensor.matmul_mx(
                out=spare[:, n, :],
                lhsT=u0[0][:].bitcast(FP8X4),
                lhsT_scale=u0[1][:],
                rhs=k_got[:, 0:P].bitcast(FP8X4),
                rhs_scale=u1[1][:],
                start=True,
                stop=True,
            )
        nc.vector.tensor_copy(k_got[:, 256:512], k_pool[:].indirect(k_list[:, 16:32]))
        c_got = sb.tile([P, SLOTS], U32, name="c_got", align_bytes=64)
        nc.vector.tensor_copy(c_got[:], c_pool[:].indirect(c_list[:]))

        v0_bf = round_queries("v0_bf", v_raw[:, 0], nc.scalar.copy)
        v0 = quantise_queries("v0", v0_bf)
        v1_bf = round_queries("v1_bf", v_raw[:, 1], nc.vector.tensor_copy, nc.scalar.copy)
        v1 = quantise_queries("v1", v1_bf)

        banks = [[psum.tile([P, hi - lo], F32, name="acc%d_%d" % (m, lo)) for lo, hi in PARTS[m]] for m in range(2)]

        def product(m, queries, got, at, first):
            codes, plane = queries
            for j, (lo, hi) in enumerate(PARTS[m]):
                nc.tensor.matmul_mx(
                    out=banks[m][j][:],
                    lhsT=codes[:].bitcast(FP8X4),
                    lhsT_scale=plane[:],
                    rhs=got[:, lo:hi].bitcast(FP8X4),
                    rhs_scale=planes[:, at + lo : at + hi],
                    start=first,
                    stop=not first,
                )

        product(0, u0, k_got, 0, True)
        product(1, u1, k_got, 0, True)
        for m, v in enumerate((v0, v1)):
            product(m, v, c_got, SLOTS, False)
            result = sb.tile([P, SLOTS], F32, name="result%d" % m, tag="late_room" if m == 0 else "result1", align_bytes=64)
            for j, (lo, hi) in enumerate(PARTS[m]):
                copy = nc.vector.tensor_copy if m == 1 and j != 1 else nc.scalar.copy
                copy(out=result[:, lo:hi], in_=banks[m][j][:])
                nc.sync.dma_start(out=out[0, m * P : (m + 1) * P, lo:hi], in_=result[:, lo:hi])
